import numpy as np
import ml_dtypes


def mxq(x, axis, fmt="e4m3"):
    dtype, down = {"e4m3": (ml_dtypes.float8_e4m3fn, 7), "e5m2": (ml_dtypes.float8_e5m2, 14)}[fmt]
    v = np.moveaxis(np.asarray(x, np.float32).astype(ml_dtypes.bfloat16).astype(np.float64), axis, -1)
    blocks = v.reshape(v.shape[:-1] + (-1, 32))
    amax = np.abs(blocks).max(-1, keepdims=True)
    byte = np.maximum(np.where(amax > 0, np.frexp(amax)[1] - 1 + 127, 0) - down, 1)
    scale = np.exp2(byte - 127.0)
    codes = (blocks / scale).astype(np.float32).astype(dtype).astype(np.float64)
    return np.moveaxis((codes * scale).reshape(v.shape), -1, axis)


WIDE = False


def mx_kscale(k):
    if not WIDE:
        return np.ones(k)
    levels = np.array([10, -10, 5, -5, 0])
    if k % 512:
        return np.exp2(np.random.permutation(np.resize(levels, k // 32))).repeat(32)
    a = np.empty((k // 512, 16))
    for p in range(k // 512):
        a[p, :8] = np.random.permutation(np.resize(levels, 8))
        for g in range(8):
            far = levels[np.abs(levels - a[p, g]) >= 10]
            a[p, g + 8] = far[np.random.randint(len(far))]
    return np.exp2(a.ravel()).repeat(32)


def f64(x):
    return np.asarray(x).astype(np.float64)


def striped(idx):
    return np.tile(idx.reshape(-1, 16).T, (8, 1)).astype(np.uint16)


def unstriped(offs):
    return offs[:16].T.reshape(-1).astype(np.int64)


def striped8(idx):
    return np.concatenate([x.reshape(-1, 16).T for x in idx]).astype(np.uint16)


def runs(offs, k):
    lists = np.stack([offs[16 * r : 16 * r + 16].T.reshape(-1) for r in range(8)]).astype(np.int64)
    return lists[np.arange(k) % 512 // 64]


def pack_weight(w):
    k, n = w.shape
    w = f64(np.asarray(w, np.float32).astype(ml_dtypes.bfloat16)).reshape(k // 32, 32, n)
    amax = np.abs(w).max(1)
    byte = np.clip(np.where(amax > 0, np.frexp(amax)[1] - 1 + 127 - 7, 1), 1, 254)
    scaled = (w * np.exp2(127.0 - byte)[:, None, :]).reshape(k, n).astype(np.float32)
    words = np.ascontiguousarray(scaled.reshape(k // 512, 128, 4, n).transpose(0, 1, 3, 2)).astype(ml_dtypes.float8_e4m3fn).view(np.uint8)
    return words, np.ascontiguousarray(byte.astype(np.uint8).reshape(k // 512, 16, n))


def unpack_weight(words, scales):
    g, p, n, _ = words.shape
    vals = np.ascontiguousarray(words).view(ml_dtypes.float8_e4m3fn).astype(np.float64) * np.repeat(np.exp2(scales.astype(np.float64) - 127.0), 8, axis=1)[..., None]
    return vals.transpose(0, 1, 3, 2).reshape(g * 512, n)


def sigmoid(v):
    return 1.0 / (1.0 + np.exp(-np.maximum(v, -700.0)))

def planes(y):
    n, m = y.shape
    v = y.astype(np.float32).astype(ml_dtypes.bfloat16).astype(np.float64).reshape(n // 32, 32, m)
    top = np.abs(v).max(1)
    byte = np.clip(np.where(top > 0, np.frexp(top)[1] - 1 + 127 - 7, 1), 1, 254)
    codes = (v * np.exp2(127.0 - byte)[:, None, :]).reshape(n, m).astype(np.float32).astype(ml_dtypes.float8_e4m3fn).view(np.uint8)
    words = codes.reshape(n // 512, 128, 4, m).transpose(0, 1, 3, 2)
    return np.ascontiguousarray(words), np.ascontiguousarray(byte.astype(np.uint8).reshape(n // 512, 16, m))


K, T, S, N, H = 512, 2048, 512, 512, 512


def setup_inputs():
    n = np.random.standard_normal
    s = mx_kscale(K)[:, None]
    u = mx_kscale(H)
    packed_xT = pack_weight(n((K, T)) * s)
    packed_w1 = pack_weight(n((K, H)) / np.sqrt(K) / s)
    packed_w2 = pack_weight(n((H, N)) / np.sqrt(2 * H) / u[:, None])
    packed_w3 = pack_weight(n((H, N)) / np.sqrt(2 * H) / u[:, None])
    return {
        "x_words": packed_xT[0],
        "x_scales": packed_xT[1],
        "w1_words": packed_w1[0],
        "w1_scales": packed_w1[1],
        "gn": (np.random.uniform(0.5, 1.5, (H, 1)) * u[:, None]).astype(np.float32),
        "gm": (np.random.uniform(0.5, 1.5, (H, 1)) * u[:, None]).astype(np.float32),
        "w2_words": packed_w2[0],
        "w2_scales": packed_w2[1],
        "w3_words": packed_w3[0],
        "w3_scales": packed_w3[1],
        "offs": striped(np.random.permutation(T)[:S]),
        "n1": striped8(np.stack([np.random.permutation(S) for _ in range(8)])),
        "n2": striped8(np.stack([np.random.permutation(S) for _ in range(8)])),
        "n3": striped8(np.stack([np.random.permutation(S) for _ in range(8)])),
        "n4": striped8(np.stack([np.random.permutation(S) for _ in range(8)])),
        "n5": striped8(np.stack([np.random.permutation(S) for _ in range(8)])),
        "n6": striped8(np.stack([np.random.permutation(S) for _ in range(8)])),
    }


def reference(x_words, x_scales, w1_words, w1_scales, gn, gm, w2_words, w2_scales, w3_words, w3_scales, offs, n1, n2, n3, n4, n5, n6):
    xq = unpack_weight(x_words, x_scales)[:, unstriped(offs)]
    y = unpack_weight(w1_words, w1_scales).T @ xq
    ex = np.exp(0.5 * y)
    z = f64(gn) * (np.log((ex + ex[np.arange(H)[:, None], runs(n1, H)]) / (ex[np.arange(H)[:, None], runs(n2, H)] + ex[np.arange(H)[:, None], runs(n3, H)])))
    st = y - (y[np.arange(H)[:, None], runs(n4, H)])
    z2 = f64(gm) * (st - (0.5 * (st[np.arange(H)[:, None], runs(n4, H)])))
    h = unpack_weight(w2_words, w2_scales).T @ mxq(z, 0, "e4m3") + unpack_weight(w3_words, w3_scales).T @ mxq(z2, 0, "e4m3")
    st2 = h * (sigmoid(h[np.arange(N)[:, None], runs(n5, N)]))
    out_0 = st2 - (st2[np.arange(N)[:, None], runs(n6, N)])
    return (out_0,) + planes(out_0)

@@ -1,0 +1,255 @@
+from contextlib import ExitStack
+
+import concourse.mybir as mybir
+from concourse.masks import make_identity
+
+K, T, S, H, N = 512, 2048, 512, 512, 512
+FLOPS = 2 * S * (K * H + 2 * H * N)
+
+F32 = mybir.dt.float32
+BF16 = mybir.dt.bfloat16
+I32 = mybir.dt.int32
+U32 = mybir.dt.uint32
+U16 = mybir.dt.uint16
+U8 = mybir.dt.uint8
+FP8X4 = mybir.dt.float8_e4m3fn_x4
+ACT = mybir.ActivationFunctionType
+ALU = mybir.AluOpType
+
+P = 128
+PACK = 4
+CHUNK = 128
+CHUNKS = S // CHUNK
+
+
+def words_of(dram):
+    return dram[0].rearrange("p n t -> p (n t)").bitcast(I32)
+
+
+def tile_picked_joinoddstwicehopg_none_po_kernel(
+    tc, x_words, x_scales, w1_words, w1_scales, gn, gm, w2_words, w2_scales, w3_words, w3_scales,
+    offs, n1, n2, n3, n4, n5, n6, out_0, out_1, out_2,
+):
+    nc = tc.nc
+    with ExitStack() as ctx:
+        lists = ctx.enter_context(tc.tile_pool(name="lists", bufs=1))
+        keep = ctx.enter_context(tc.tile_pool(name="keep", bufs=1))
+        psum = ctx.enter_context(tc.psum_pool(name="psum", bufs=1))
+
+        def sb(name, shape, dtype):
+            return keep.tile(shape, dtype, name=name, align_bytes=64)
+
+        def bank(index, name):
+            return psum.tile([P, 512], F32, name=name, tag="bank%d" % index)
+
+        def load_list(name, dram):
+            held = lists.tile([P, S // 16], U16, name=name)
+            nc.sync.dma_start(held[:], dram)
+            return held
+
+        def load_scales(queue, plane, first_row, dram):
+            for q in range(4):
+                rows = slice(32 * q + first_row, 32 * q + first_row + 4)
+                queue.dma_start(plane[rows, :].bitcast(I32), dram[0, 4 * q : 4 * q + 4, :].bitcast(I32))
+
+        def deal(dealt, raw):
+            nc.vector.tensor_copy(
+                out=dealt.rearrange("p (t m) -> p m t", t=PACK), in_=raw.rearrange("p (m t) -> p m t", t=PACK)
+            )
+
+        def deal_words(dealt, raw):
+            nc.vector.tensor_copy(
+                out=dealt.rearrange("p (t m) -> p t m", t=PACK), in_=raw.rearrange("p (m t) -> p t m", t=PACK)
+            )
+
+        x_scale_table = sb("x_scale_table", [P, T], U8)
+        w1_scale_raw = sb("w1_scale_raw", [P, H], U8)
+        w23_scale_raw = sb("w23_scale_raw", [P, N], U8)
+        nc.gpsimd.memset(x_scale_table[:].bitcast(I32), 0)
+        ident = sb("ident", [P, P], F32)
+        make_identity(nc, ident[:])
+        nc.vector.memset(w1_scale_raw[:].bitcast(I32), 0)
+        nc.vector.memset(w23_scale_raw[:].bitcast(I32), 0)
+
+        picks = load_list("picks", offs)
+        x_table = sb("x_table", [P, T], I32)
+        nc.sync.dma_start(x_table[:], words_of(x_words))
+        load_scales(nc.scalar, x_scale_table, 0, x_scales)
+        w1_raw = sb("w1_raw", [P, H], I32)
+        nc.sync.dma_start(w1_raw[:], words_of(w1_words))
+        load_scales(nc.scalar, w1_scale_raw, 0, w1_scales)
+        list4 = load_list("list4", n4)
+        list1 = load_list("list1", n1)
+        list2 = load_list("list2", n2)
+        list3 = load_list("list3", n3)
+        w2_raw = sb("w2_raw", [P, N], I32)
+        w3_raw = sb("w3_raw", [P, N], I32)
+        nc.sync.dma_start(w2_raw[:], words_of(w2_words))
+        nc.sync.dma_start(w3_raw[:], words_of(w3_words))
+        gn_cols = sb("gn_cols", [P, PACK], F32)
+        gm_cols = sb("gm_cols", [P, PACK], F32)
+        nc.gpsimd.dma_start(gm_cols[:], gm.rearrange("(p t) o -> p (t o)", t=PACK))
+        nc.gpsimd.dma_start(gn_cols[:], gn.rearrange("(p t) o -> p (t o)", t=PACK))
+        list5 = load_list("list5", n5)
+        list6 = load_list("list6", n6)
+        load_scales(nc.sync, w23_scale_raw, 0, w2_scales)
+        load_scales(nc.sync, w23_scale_raw, 4, w3_scales)
+
+        win_a = [sb("win_a%d" % t, [P, 2 * S], F32) for t in range(PACK)]
+        win_b = [sb("win_b%d" % t, [P, 2 * S], F32) for t in range(PACK)]
+        for t in range(PACK):
+            nc.vector.memset(win_b[t][:, S:], 0.0)
+
+        w1_codes = sb("w1_codes", [P, H], I32)
+        w1_plane = sb("w1_plane", [P, H], U8)
+        deal_words(w1_codes[:], w1_raw[:])
+        deal(w1_plane[:], w1_scale_raw[:])
+
+        x_codes = sb("x_codes", [P, S], U32)
+        x_plane = sb("x_plane", [P, S], U8)
+        nc.vector.tensor_copy(x_plane[:], x_scale_table[:].indirect(picks[:]))
+        nc.vector.tensor_copy(x_codes[:], x_table[:].bitcast(U32).indirect(picks[:]))
+
+        y_bank = [bank(t, "y_bank%d" % t) for t in range(PACK)]
+        for t in range(PACK):
+            rows = slice(t * P, (t + 1) * P)
+            nc.tensor.matmul_mx(
+                out=y_bank[t][:], lhsT=w1_codes[:, rows].bitcast(FP8X4), lhsT_scale=w1_plane[:, rows],
+                rhs=x_codes[:].bitcast(FP8X4), rhs_scale=x_plane[:], start=True, stop=True,
+            )
+
+        w2_codes = sb("w2_codes", [P, N], I32)
+        w3_codes = sb("w3_codes", [P, N], I32)
+        w23_plane = sb("w23_plane", [P, N], U8)
+        deal_words(w2_codes[:], w2_raw[:])
+        deal_words(w3_codes[:], w3_raw[:])
+
+        gn_wide = sb("gn_wide", [P, PACK, CHUNK], F32)
+        for t in range(PACK):
+            nc.vector.tensor_copy(gn_wide[:, t, :], gn_cols[:, t : t + 1].to_broadcast([P, CHUNK]))
+        gm_bank = bank(4, "gm_bank")
+        for t in range(PACK):
+            nc.tensor.transpose(gm_bank[:, t * P : (t + 1) * P], gm_cols[:, t : t + 1].to_broadcast([P, P]), ident[:])
+        gm_row = sb("gm_row", [P, 2, P, 2], F32)
+        nc.scalar.copy(gm_row[:], gm_bank[:].rearrange("j (u e p) -> j u p e", u=2, e=2))
+
+        sums = sb("sums", [P, 2 * PACK, S], F32)
+        z2t_bank = [bank(4 + c, "z2t_bank%d" % c) for c in range(CHUNKS)]
+        for t in range(PACK):
+            y_t = win_a[t][:, :S]
+            ex_t = win_a[t][:, S:]
+            if t < 3:
+                nc.vector.tensor_copy(y_t, y_bank[t][:])
+            else:
+                nc.scalar.copy(y_t, y_bank[t][:])
+            nc.scalar.activation(ex_t, y_bank[t][:], ACT.Exp, scale=0.5)
+            ex1 = sb("ex1_%d" % t, [P, S], F32)
+            ex2 = sb("ex2_%d" % t, [P, S], F32)
+            ex3 = sb("ex3_%d" % t, [P, S], F32)
+            nc.scalar.activation(ex1[:], win_a[t][:].indirect(list1[:]), ACT.Exp, scale=0.5)
+            nc.scalar.activation(ex2[:], win_a[t][:].indirect(list2[:]), ACT.Exp, scale=0.5)
+            nc.scalar.activation(ex3[:], win_a[t][:].indirect(list3[:]), ACT.Exp, scale=0.5)
+
+            hop1 = win_b[t][:, :S]
+            hop2 = sb("hop2_%d" % t, [P, S], F32)
+            nc.vector.tensor_scalar(hop1, win_a[t][:].indirect(list4[:]), -1.5, 0.0, ALU.mult, ALU.add)
+            nc.vector.tensor_scalar(hop2[:], win_b[t][:].indirect(list4[:]), -1.0 / 3.0, 0.0, ALU.mult, ALU.add)
+            terms = (y_t, hop1, hop2[:])
+            for i in range(3):
+                for c in range(CHUNKS):
+                    nc.tensor.matmul(
+                        z2t_bank[c][:, t * P : (t + 1) * P], terms[i][:, c * CHUNK : (c + 1) * CHUNK], ident[:],
+                        start=(i == 0), stop=(i == 2), is_transpose=True,
+                    )
+            nc.vector.tensor_tensor(sums[:, t, :], ex_t, ex1[:], ALU.add)
+            nc.vector.tensor_tensor(sums[:, PACK + t, :], ex2[:], ex3[:], ALU.add)
+
+        deal(w23_plane[:], w23_scale_raw[:])
+        z2_bf = sb("z2_bf", [P, S * PACK], BF16)
+        z2_codes = sb("z2_codes", [P, S], U32)
+        z2_plane = sb("z2_plane", [P, S], U8)
+        z2t = [sb("z2t%d" % c, [P, 2, P, 2], BF16) for c in range(CHUNKS)]
+        for c in range(CHUNKS):
+            nc.vector.tensor_tensor(
+                z2t[c][:], z2t_bank[c][:].rearrange("j (u e p) -> j u p e", u=2, e=2), gm_row[:], ALU.mult
+            )
+        for half in range(2):
+            word_bank = bank(4 + 2 * half, "word_bank%d" % half)
+            for c in range(2):
+                pairs = z2t[2 * half + c][:].rearrange("j u p e -> j (u p e)").bitcast(F32)
+                for u in range(2):
+                    at = (2 * c + u) * P
+                    nc.tensor.transpose(word_bank[:, at : at + P], pairs[:, u * P : (u + 1) * P], ident[:])
+            wide = slice(half * 1024, (half + 1) * 1024)
+            cols = slice(half * 256, (half + 1) * 256)
+            nc.scalar.copy(
+                z2_bf[:, wide].bitcast(F32).rearrange("p (c j u) -> p c j u", c=2, u=2),
+                word_bank[:].rearrange("p (c u j) -> p c j u", c=2, u=2),
+            )
+            nc.vector.quantize_mx(out=z2_codes[:, cols].bitcast(FP8X4), scales=z2_plane[:, cols], in_=z2_bf[:, wide])
+
+        z_bf = sb("z_bf", [P, S * PACK], BF16)
+        z_codes = sb("z_codes", [P, S], U32)
+        z_plane = sb("z_plane", [P, S], U8)
+        h_bank = [bank(t, "h_bank%d" % t) for t in range(PACK)]
+        for c in range(CHUNKS):
+            cols = slice(c * CHUNK, (c + 1) * CHUNK)
+            wide = slice(c * CHUNK * PACK, (c + 1) * CHUNK * PACK)
+            logs = sb("logs%d" % c, [P, 2 * PACK, CHUNK], F32)
+            nc.scalar.activation(logs[:], sums[:, :, cols], ACT.Ln)
+            odds = sb("odds%d" % c, [P, PACK, CHUNK], F32)
+            nc.vector.tensor_tensor(odds[:], logs[:, :PACK, :], logs[:, PACK:, :], ALU.subtract)
+            nc.vector.tensor_tensor(
+                z_bf[:, wide].rearrange("p (c i t) -> p c t i", i=4, t=PACK),
+                odds[:].rearrange("p t (c i) -> p c t i", i=4),
+                gn_wide[:].rearrange("p t (c i) -> p c t i", i=4),
+                ALU.mult,
+            )
+            nc.vector.quantize_mx(out=z_codes[:, cols].bitcast(FP8X4), scales=z_plane[:, cols], in_=z_bf[:, wide])
+            for t in range(PACK):
+                rows = slice(t * P, (t + 1) * P)
+                nc.tensor.matmul_mx(
+                    out=h_bank[t][:, cols], lhsT=w3_codes[:, rows].bitcast(FP8X4), lhsT_scale=w23_plane[4:, rows],
+                    rhs=z2_codes[:, cols].bitcast(FP8X4), rhs_scale=z2_plane[:, cols], start=True, stop=False,
+                )
+                nc.tensor.matmul_mx(
+                    out=h_bank[t][:, cols], lhsT=w2_codes[:, rows].bitcast(FP8X4), lhsT_scale=w23_plane[:, rows],
+                    rhs=z_codes[:, cols].bitcast(FP8X4), rhs_scale=z_plane[:, cols], start=False, stop=True,
+                )
+
+        result = sb("result", [P, PACK, S], F32)
+        out_rows = out_0.rearrange("(p t) j -> p t j", t=PACK)
+        out_bf = sb("out_bf", [P, S * PACK], BF16)
+        out_codes = sb("out_codes", [P, S], U32)
+        out_plane = sb("out_plane", [P, S], U8)
+        half = S // 2
+        for t in range(2):
+            nc.vector.tensor_copy(win_a[t][:, :S], h_bank[t][:])
+        for t in range(PACK):
+            if t < 2:
+                gate = win_a[t + 2][:, :S]
+            else:
+                nc.scalar.copy(win_a[t][:, :S], h_bank[t][:])
+                gate = win_a[t - 2][:, :S]
+            nc.scalar.activation(gate, win_a[t][:].indirect(list5[:]), ACT.Sigmoid)
+            st2 = win_b[t][:, :S]
+            nc.vector.tensor_tensor(st2, h_bank[t][:], gate, ALU.mult)
+            other = sb("other%d" % t, [P, S], F32)
+            for lo, hi in ((0, S),) if t < PACK - 1 else ((0, half), (half, S)):
+                nc.vector.tensor_copy(other[:, lo:hi], win_b[t][:].indirect(list6[:, lo // 16 : hi // 16]))
+                nc.vector.tensor_tensor(result[:, t, lo:hi], st2[:, lo:hi], other[:, lo:hi], ALU.subtract)
+                nc.sync.dma_start(out_rows[:, t, lo:hi], result[:, t, lo:hi])
+
+        for copy, lo, hi in ((nc.scalar.copy, 0, half), (nc.vector.tensor_copy, half, S)):
+            copy(
+                out_bf[:, lo * PACK : hi * PACK].rearrange("p (c i t) -> p c t i", i=4, t=PACK),
+                result[:, :, lo:hi].rearrange("p t (c i) -> p c t i", i=4),
+            )
+        for lo, hi in ((0, half), (half, S)):
+            nc.vector.quantize_mx(
+                out=out_codes[:, lo:hi].bitcast(FP8X4), scales=out_plane[:, lo:hi], in_=out_bf[:, lo * PACK : hi * PACK]
+            )
+            nc.scalar.dma_start(words_of(out_1)[:, lo:hi], out_codes[:, lo:hi].bitcast(I32))
+        for q in range(4):
+            queue = nc.scalar if q % 2 else nc.sync
+            queue.dma_start(out_2[0, 4 * q : 4 * q + 4, :].bitcast(I32), out_plane[32 * q : 32 * q + 4, :].bitcast(I32))

@@ -20,6 +20,7 @@ P = 128
 PACK = 4
 CHUNK = 128
 CHUNKS = S // CHUNK
+SHARED = 2
 
 
 def words_of(dram):
@@ -57,27 +58,27 @@ def tile_picked_joinoddstwicehopg_none_po_kernel(
                 out=dealt.rearrange("p (t m) -> p m t", t=PACK), in_=raw.rearrange("p (m t) -> p m t", t=PACK)
             )
 
-        def deal_words(dealt, raw):
-            nc.vector.tensor_copy(
+        def deal_words(engine, dealt, raw):
+            engine.tensor_copy(
                 out=dealt.rearrange("p (t m) -> p t m", t=PACK), in_=raw.rearrange("p (m t) -> p t m", t=PACK)
             )
 
         x_scale_table = sb("x_scale_table", [P, T], U8)
         w1_scale_raw = sb("w1_scale_raw", [P, H], U8)
         w23_scale_raw = sb("w23_scale_raw", [P, N], U8)
-        nc.gpsimd.memset(x_scale_table[:].bitcast(I32), 0)
-        ident = sb("ident", [P, P], F32)
-        make_identity(nc, ident[:])
+        nc.vector.memset(x_scale_table[:].bitcast(I32), 0)
         nc.vector.memset(w1_scale_raw[:].bitcast(I32), 0)
         nc.vector.memset(w23_scale_raw[:].bitcast(I32), 0)
+        ident = sb("ident", [P, P], F32)
+        make_identity(nc, ident[:])
 
         picks = load_list("picks", offs)
         x_table = sb("x_table", [P, T], I32)
         nc.sync.dma_start(x_table[:], words_of(x_words))
-        load_scales(nc.scalar, x_scale_table, 0, x_scales)
+        load_scales(nc.sync, x_scale_table, 0, x_scales)
         w1_raw = sb("w1_raw", [P, H], I32)
         nc.sync.dma_start(w1_raw[:], words_of(w1_words))
-        load_scales(nc.scalar, w1_scale_raw, 0, w1_scales)
+        load_scales(nc.sync, w1_scale_raw, 0, w1_scales)
         list4 = load_list("list4", n4)
         list1 = load_list("list1", n1)
         list2 = load_list("list2", n2)
@@ -97,12 +98,16 @@ def tile_picked_joinoddstwicehopg_none_po_kernel(
 
         win_a = [sb("win_a%d" % t, [P, 2 * S], F32) for t in range(PACK)]
         win_b = [sb("win_b%d" % t, [P, 2 * S], F32) for t in range(PACK)]
+        win_e = [sb("win_e%d" % t, [P, 2 * S], F32) for t in range(SHARED)]
+        for t in range(SHARED):
+            nc.vector.memset(win_a[t][:, S:], 0.0)
+            nc.vector.memset(win_e[t][:, S:], 0.0)
         for t in range(PACK):
-            nc.vector.memset(win_b[t][:, S:], 0.0)
+            nc.gpsimd.memset(win_b[t][:, S:], 0.0)
 
         w1_codes = sb("w1_codes", [P, H], I32)
         w1_plane = sb("w1_plane", [P, H], U8)
-        deal_words(w1_codes[:], w1_raw[:])
+        deal_words(nc.vector, w1_codes[:], w1_raw[:])
         deal(w1_plane[:], w1_scale_raw[:])
 
         x_codes = sb("x_codes", [P, S], U32)
@@ -121,8 +126,8 @@ def tile_picked_joinoddstwicehopg_none_po_kernel(
         w2_codes = sb("w2_codes", [P, N], I32)
         w3_codes = sb("w3_codes", [P, N], I32)
         w23_plane = sb("w23_plane", [P, N], U8)
-        deal_words(w2_codes[:], w2_raw[:])
-        deal_words(w3_codes[:], w3_raw[:])
+        deal_words(nc.vector, w2_codes[:], w2_raw[:])
+        deal_words(nc.vector, w3_codes[:], w3_raw[:])
 
         gn_wide = sb("gn_wide", [P, PACK, CHUNK], F32)
         for t in range(PACK):
@@ -135,36 +140,62 @@ def tile_picked_joinoddstwicehopg_none_po_kernel(
 
         sums = sb("sums", [P, 2 * PACK, S], F32)
         z2t_bank = [bank(4 + c, "z2t_bank%d" % c) for c in range(CHUNKS)]
-        for t in range(PACK):
-            y_t = win_a[t][:, :S]
-            ex_t = win_a[t][:, S:]
-            if t < 3:
-                nc.vector.tensor_copy(y_t, y_bank[t][:])
-            else:
-                nc.scalar.copy(y_t, y_bank[t][:])
-            nc.scalar.activation(ex_t, y_bank[t][:], ACT.Exp, scale=0.5)
-            ex1 = sb("ex1_%d" % t, [P, S], F32)
-            ex2 = sb("ex2_%d" % t, [P, S], F32)
-            ex3 = sb("ex3_%d" % t, [P, S], F32)
-            nc.scalar.activation(ex1[:], win_a[t][:].indirect(list1[:]), ACT.Exp, scale=0.5)
-            nc.scalar.activation(ex2[:], win_a[t][:].indirect(list2[:]), ACT.Exp, scale=0.5)
-            nc.scalar.activation(ex3[:], win_a[t][:].indirect(list3[:]), ACT.Exp, scale=0.5)
+        ex1 = [sb("ex1_%d" % t, [P, S], F32) for t in range(PACK)]
+        ex2 = [sb("ex2_%d" % t, [P, S], F32) for t in range(PACK)]
+        ex3 = [sb("ex3_%d" % t, [P, S], F32) for t in range(PACK)]
+        hop2 = [sb("hop2_%d" % t, [P, S], F32) for t in range(PACK)]
+        ex = [win_e[t][:, :S] if t < SHARED else win_a[t][:, S:] for t in range(PACK)]
 
-            hop1 = win_b[t][:, :S]
-            hop2 = sb("hop2_%d" % t, [P, S], F32)
-            nc.vector.tensor_scalar(hop1, win_a[t][:].indirect(list4[:]), -1.5, 0.0, ALU.mult, ALU.add)
-            nc.vector.tensor_scalar(hop2[:], win_b[t][:].indirect(list4[:]), -1.0 / 3.0, 0.0, ALU.mult, ALU.add)
-            terms = (y_t, hop1, hop2[:])
-            for i in range(3):
-                for c in range(CHUNKS):
-                    nc.tensor.matmul(
-                        z2t_bank[c][:, t * P : (t + 1) * P], terms[i][:, c * CHUNK : (c + 1) * CHUNK], ident[:],
-                        start=(i == 0), stop=(i == 2), is_transpose=True,
-                    )
-            nc.vector.tensor_tensor(sums[:, t, :], ex_t, ex1[:], ALU.add)
-            nc.vector.tensor_tensor(sums[:, PACK + t, :], ex2[:], ex3[:], ALU.add)
+        def copy_y(t):
+            nc.vector.tensor_copy(win_a[t][:, :S], y_bank[t][:])
+
+        def scalar_side(t):
+            nc.scalar.activation(ex[t], y_bank[t][:], ACT.Exp, scale=0.5)
+            nc.scalar.activation(ex1[t][:], win_a[t][:].indirect(list1[:]), ACT.Exp, scale=0.5)
+            nc.scalar.activation(ex2[t][:], win_a[t][:].indirect(list2[:]), ACT.Exp, scale=0.5)
+            if t >= SHARED:
+                nc.scalar.activation(ex3[t][:], win_a[t][:].indirect(list3[:]), ACT.Exp, scale=0.5)
+
+        def turn(term, t, first, last):
+            for c in range(CHUNKS):
+                nc.tensor.matmul(
+                    z2t_bank[c][:, t * P : (t + 1) * P], term[:, c * CHUNK : (c + 1) * CHUNK], ident[:],
+                    start=first, stop=last, is_transpose=True,
+                )
+
+        def first_hop(t):
+            nc.vector.tensor_scalar(win_b[t][:, :S], win_a[t][:].indirect(list4[:]), -1.5, 0.0, ALU.mult, ALU.add)
+
+        def second_hop(t):
+            nc.vector.tensor_scalar(hop2[t][:], win_b[t][:].indirect(list4[:]), -1.0 / 3.0, 0.0, ALU.mult, ALU.add)
+            turn(win_a[t][:, :S], t, True, False)
+            turn(win_b[t][:, :S], t, False, False)
+            turn(hop2[t][:], t, False, True)
+
+        def add_up(t):
+            nc.gpsimd.tensor_tensor(sums[:, t, :], ex[t], ex1[t][:], ALU.add)
+            nc.gpsimd.tensor_tensor(sums[:, PACK + t, :], ex2[t][:], ex3[t][:], ALU.add)
+
+        copy_y(0)
+        copy_y(1)
+        for t in range(SHARED):
+            scalar_side(t)
+            first_hop(t)
+            nc.vector.tensor_copy(ex3[t][:], win_e[t][:].indirect(list3[:]))
+            second_hop(t)
+            copy_y(t + 2)
+            add_up(t)
+        for t in range(SHARED, PACK):
+            scalar_side(t)
+            first_hop(t)
+        for t in range(SHARED, PACK):
+            second_hop(t)
+            add_up(t)
 
         deal(w23_plane[:], w23_scale_raw[:])
+        warm = sb("warm", [P, 2], F32)
+        nc.scalar.activation(warm[:, 0:1], ex3[PACK - 1][:, 0:1], ACT.Ln)
+
         z2_bf = sb("z2_bf", [P, S * PACK], BF16)
         z2_codes = sb("z2_codes", [P, S], U32)
         z2_plane = sb("z2_plane", [P, S], U8)
@@ -173,7 +204,8 @@ def tile_picked_joinoddstwicehopg_none_po_kernel(
             nc.vector.tensor_tensor(
                 z2t[c][:], z2t_bank[c][:].rearrange("j (u e p) -> j u p e", u=2, e=2), gm_row[:], ALU.mult
             )
-        for half in range(2):
+
+        def turn_back(half):
             word_bank = bank(4 + 2 * half, "word_bank%d" % half)
             for c in range(2):
                 pairs = z2t[2 * half + c][:].rearrange("j u p e -> j (u p e)").bitcast(F32)
@@ -181,30 +213,40 @@ def tile_picked_joinoddstwicehopg_none_po_kernel(
                     at = (2 * c + u) * P
                     nc.tensor.transpose(word_bank[:, at : at + P], pairs[:, u * P : (u + 1) * P], ident[:])
             wide = slice(half * 1024, (half + 1) * 1024)
-            cols = slice(half * 256, (half + 1) * 256)
             nc.scalar.copy(
                 z2_bf[:, wide].bitcast(F32).rearrange("p (c j u) -> p c j u", c=2, u=2),
                 word_bank[:].rearrange("p (c u j) -> p c j u", c=2, u=2),
             )
+
+        def quantize_z2(half):
+            wide = slice(half * 1024, (half + 1) * 1024)
+            cols = slice(half * 256, (half + 1) * 256)
             nc.vector.quantize_mx(out=z2_codes[:, cols].bitcast(FP8X4), scales=z2_plane[:, cols], in_=z2_bf[:, wide])
 
         z_bf = sb("z_bf", [P, S * PACK], BF16)
         z_codes = sb("z_codes", [P, S], U32)
         z_plane = sb("z_plane", [P, S], U8)
         h_bank = [bank(t, "h_bank%d" % t) for t in range(PACK)]
-        for c in range(CHUNKS):
-            cols = slice(c * CHUNK, (c + 1) * CHUNK)
-            wide = slice(c * CHUNK * PACK, (c + 1) * CHUNK * PACK)
-            logs = sb("logs%d" % c, [P, 2 * PACK, CHUNK], F32)
-            nc.scalar.activation(logs[:], sums[:, :, cols], ACT.Ln)
-            odds = sb("odds%d" % c, [P, PACK, CHUNK], F32)
-            nc.vector.tensor_tensor(odds[:], logs[:, :PACK, :], logs[:, PACK:, :], ALU.subtract)
+        logs = [sb("logs%d" % c, [P, 2 * PACK, CHUNK], F32) for c in range(CHUNKS)]
+        odds = [sb("odds%d" % c, [P, PACK, CHUNK], F32) for c in range(CHUNKS)]
+
+        def take_logs(c):
+            nc.scalar.activation(logs[c][:], sums[:, :, c * CHUNK : (c + 1) * CHUNK], ACT.Ln)
+
+        def subtract_logs(c):
+            nc.vector.tensor_tensor(odds[c][:], logs[c][:, :PACK, :], logs[c][:, PACK:, :], ALU.subtract)
+
+        def gain_z(c):
             nc.vector.tensor_tensor(
-                z_bf[:, wide].rearrange("p (c i t) -> p c t i", i=4, t=PACK),
-                odds[:].rearrange("p t (c i) -> p c t i", i=4),
+                z_bf[:, c * CHUNK * PACK : (c + 1) * CHUNK * PACK].rearrange("p (c i t) -> p c t i", i=4, t=PACK),
+                odds[c][:].rearrange("p t (c i) -> p c t i", i=4),
                 gn_wide[:].rearrange("p t (c i) -> p c t i", i=4),
                 ALU.mult,
             )
+
+        def multiply(c):
+            cols = slice(c * CHUNK, (c + 1) * CHUNK)
+            wide = slice(c * CHUNK * PACK, (c + 1) * CHUNK * PACK)
             nc.vector.quantize_mx(out=z_codes[:, cols].bitcast(FP8X4), scales=z_plane[:, cols], in_=z_bf[:, wide])
             for t in range(PACK):
                 rows = slice(t * P, (t + 1) * P)
@@ -217,6 +259,28 @@ def tile_picked_joinoddstwicehopg_none_po_kernel(
                     rhs=z_codes[:, cols].bitcast(FP8X4), rhs_scale=z_plane[:, cols], start=False, stop=True,
                 )
 
+        take_logs(0)
+        turn_back(0)
+        subtract_logs(0)
+        take_logs(1)
+        quantize_z2(0)
+        gain_z(0)
+        turn_back(1)
+        subtract_logs(1)
+        multiply(0)
+        take_logs(2)
+        gain_z(1)
+        quantize_z2(1)
+        multiply(1)
+        subtract_logs(2)
+        take_logs(3)
+        gain_z(2)
+        subtract_logs(3)
+        multiply(2)
+        gain_z(3)
+        multiply(3)
+
+        nc.scalar.activation(warm[:, 1:2], logs[CHUNKS - 1][:, 0, 0:1], ACT.Sigmoid)
         result = sb("result", [P, PACK, S], F32)
         out_rows = out_0.rearrange("(p t) j -> p t j", t=PACK)
         out_bf = sb("out_bf", [P, S * PACK], BF16)
@@ -237,7 +301,7 @@ def tile_picked_joinoddstwicehopg_none_po_kernel(
             other = sb("other%d" % t, [P, S], F32)
             for lo, hi in ((0, S),) if t < PACK - 1 else ((0, half), (half, S)):
                 nc.vector.tensor_copy(other[:, lo:hi], win_b[t][:].indirect(list6[:, lo // 16 : hi // 16]))
-                nc.vector.tensor_tensor(result[:, t, lo:hi], st2[:, lo:hi], other[:, lo:hi], ALU.subtract)
+                (nc.gpsimd if t < PACK - 1 else nc.vector).tensor_tensor(result[:, t, lo:hi], st2[:, lo:hi], other[:, lo:hi], ALU.subtract)
                 nc.sync.dma_start(out_rows[:, t, lo:hi], result[:, t, lo:hi])
 
         for copy, lo, hi in ((nc.scalar.copy, 0, half), (nc.vector.tensor_copy, half, S)):

@@ -20,11 +20,21 @@ P = 128
 PACK = 4
 CHUNK = 128
 CHUNKS = S // CHUNK
+HALF = S // 2
+RUN = 4
 SHARED = 2
 
 
 def words_of(dram):
     return dram[0].rearrange("p n t -> p (n t)").bitcast(I32)
+
+
+def interleaved(tile):
+    return tile.rearrange("p (c i t) -> p c t i", i=RUN, t=PACK)
+
+
+def by_runs(quarters):
+    return quarters.rearrange("p t (c i) -> p c t i", i=RUN)
 
 
 def tile_picked_joinoddstwicehopg_none_po_kernel(
@@ -37,8 +47,8 @@ def tile_picked_joinoddstwicehopg_none_po_kernel(
         keep = ctx.enter_context(tc.tile_pool(name="keep", bufs=1))
         psum = ctx.enter_context(tc.psum_pool(name="psum", bufs=1))
 
-        def sb(name, shape, dtype):
-            return keep.tile(shape, dtype, name=name, align_bytes=64)
+        def sb(name, shape, dtype, tag=""):
+            return keep.tile(shape, dtype, name=name, tag=tag or name, align_bytes=64)
 
         def bank(index, name):
             return psum.tile([P, 512], F32, name=name, tag="bank%d" % index)
@@ -48,19 +58,19 @@ def tile_picked_joinoddstwicehopg_none_po_kernel(
             nc.sync.dma_start(held[:], dram)
             return held
 
-        def load_scales(queue, plane, first_row, dram):
+        def load_scales(tile, first_row, dram):
             for q in range(4):
                 rows = slice(32 * q + first_row, 32 * q + first_row + 4)
-                queue.dma_start(plane[rows, :].bitcast(I32), dram[0, 4 * q : 4 * q + 4, :].bitcast(I32))
+                nc.sync.dma_start(tile[rows, :].bitcast(I32), dram[0, 4 * q : 4 * q + 4, :].bitcast(I32))
 
         def deal(dealt, raw):
             nc.vector.tensor_copy(
-                out=dealt.rearrange("p (t m) -> p m t", t=PACK), in_=raw.rearrange("p (m t) -> p m t", t=PACK)
+                out=dealt.rearrange("p (t m) -> p t m", t=PACK), in_=raw.rearrange("p (m t) -> p t m", t=PACK)
             )
 
-        def deal_words(engine, dealt, raw):
-            engine.tensor_copy(
-                out=dealt.rearrange("p (t m) -> p t m", t=PACK), in_=raw.rearrange("p (m t) -> p t m", t=PACK)
+        def deal_bytes(dealt, raw):
+            nc.vector.tensor_copy(
+                out=dealt.rearrange("p (t m) -> p m t", t=PACK), in_=raw.rearrange("p (m t) -> p m t", t=PACK)
             )
 
         x_scale_table = sb("x_scale_table", [P, T], U8)
@@ -75,10 +85,10 @@ def tile_picked_joinoddstwicehopg_none_po_kernel(
         picks = load_list("picks", offs)
         x_table = sb("x_table", [P, T], I32)
         nc.sync.dma_start(x_table[:], words_of(x_words))
-        load_scales(nc.sync, x_scale_table, 0, x_scales)
+        load_scales(x_scale_table, 0, x_scales)
         w1_raw = sb("w1_raw", [P, H], I32)
         nc.sync.dma_start(w1_raw[:], words_of(w1_words))
-        load_scales(nc.sync, w1_scale_raw, 0, w1_scales)
+        load_scales(w1_scale_raw, 0, w1_scales)
         list4 = load_list("list4", n4)
         list1 = load_list("list1", n1)
         list2 = load_list("list2", n2)
@@ -93,8 +103,8 @@ def tile_picked_joinoddstwicehopg_none_po_kernel(
         nc.gpsimd.dma_start(gn_cols[:], gn.rearrange("(p t) o -> p (t o)", t=PACK))
         list5 = load_list("list5", n5)
         list6 = load_list("list6", n6)
-        load_scales(nc.sync, w23_scale_raw, 0, w2_scales)
-        load_scales(nc.sync, w23_scale_raw, 4, w3_scales)
+        load_scales(w23_scale_raw, 0, w2_scales)
+        load_scales(w23_scale_raw, 4, w3_scales)
 
         win_a = [sb("win_a%d" % t, [P, 2 * S], F32) for t in range(PACK)]
         win_b = [sb("win_b%d" % t, [P, 2 * S], F32) for t in range(PACK)]
@@ -106,28 +116,28 @@ def tile_picked_joinoddstwicehopg_none_po_kernel(
             nc.gpsimd.memset(win_b[t][:, S:], 0.0)
 
         w1_codes = sb("w1_codes", [P, H], I32)
-        w1_plane = sb("w1_plane", [P, H], U8)
-        deal_words(nc.vector, w1_codes[:], w1_raw[:])
-        deal(w1_plane[:], w1_scale_raw[:])
+        w1_bytes = sb("w1_bytes", [P, H], U8)
+        deal(w1_codes[:], w1_raw[:])
+        deal_bytes(w1_bytes[:], w1_scale_raw[:])
 
         x_codes = sb("x_codes", [P, S], U32)
-        x_plane = sb("x_plane", [P, S], U8)
-        nc.vector.tensor_copy(x_plane[:], x_scale_table[:].indirect(picks[:]))
+        x_bytes = sb("x_bytes", [P, S], U8)
+        nc.vector.tensor_copy(x_bytes[:], x_scale_table[:].indirect(picks[:]))
         nc.vector.tensor_copy(x_codes[:], x_table[:].bitcast(U32).indirect(picks[:]))
 
         y_bank = [bank(t, "y_bank%d" % t) for t in range(PACK)]
         for t in range(PACK):
             rows = slice(t * P, (t + 1) * P)
             nc.tensor.matmul_mx(
-                out=y_bank[t][:], lhsT=w1_codes[:, rows].bitcast(FP8X4), lhsT_scale=w1_plane[:, rows],
-                rhs=x_codes[:].bitcast(FP8X4), rhs_scale=x_plane[:], start=True, stop=True,
+                out=y_bank[t][:], lhsT=w1_codes[:, rows].bitcast(FP8X4), lhsT_scale=w1_bytes[:, rows],
+                rhs=x_codes[:].bitcast(FP8X4), rhs_scale=x_bytes[:], start=True, stop=True,
             )
 
         w2_codes = sb("w2_codes", [P, N], I32)
         w3_codes = sb("w3_codes", [P, N], I32)
-        w23_plane = sb("w23_plane", [P, N], U8)
-        deal_words(nc.vector, w2_codes[:], w2_raw[:])
-        deal_words(nc.vector, w3_codes[:], w3_raw[:])
+        w23_bytes = sb("w23_bytes", [P, N], U8)
+        deal(w2_codes[:], w2_raw[:])
+        deal(w3_codes[:], w3_raw[:])
 
         gn_wide = sb("gn_wide", [P, PACK, CHUNK], F32)
         for t in range(PACK):
@@ -139,7 +149,7 @@ def tile_picked_joinoddstwicehopg_none_po_kernel(
         nc.scalar.copy(gm_row[:], gm_bank[:].rearrange("j (u e p) -> j u p e", u=2, e=2))
 
         sums = sb("sums", [P, 2 * PACK, S], F32)
-        z2t_bank = [bank(4 + c, "z2t_bank%d" % c) for c in range(CHUNKS)]
+        turned_bank = [bank(PACK + c, "turned_bank%d" % c) for c in range(CHUNKS)]
         ex1 = [sb("ex1_%d" % t, [P, S], F32) for t in range(PACK)]
         ex2 = [sb("ex2_%d" % t, [P, S], F32) for t in range(PACK)]
         ex3 = [sb("ex3_%d" % t, [P, S], F32) for t in range(PACK)]
@@ -149,17 +159,17 @@ def tile_picked_joinoddstwicehopg_none_po_kernel(
         def copy_y(t):
             nc.vector.tensor_copy(win_a[t][:, :S], y_bank[t][:])
 
-        def scalar_side(t):
+        def exponentials(t):
             nc.scalar.activation(ex[t], y_bank[t][:], ACT.Exp, scale=0.5)
             nc.scalar.activation(ex1[t][:], win_a[t][:].indirect(list1[:]), ACT.Exp, scale=0.5)
             nc.scalar.activation(ex2[t][:], win_a[t][:].indirect(list2[:]), ACT.Exp, scale=0.5)
             if t >= SHARED:
                 nc.scalar.activation(ex3[t][:], win_a[t][:].indirect(list3[:]), ACT.Exp, scale=0.5)
 
-        def turn(term, t, first, last):
+        def turn_and_add(term, t, first, last):
             for c in range(CHUNKS):
                 nc.tensor.matmul(
-                    z2t_bank[c][:, t * P : (t + 1) * P], term[:, c * CHUNK : (c + 1) * CHUNK], ident[:],
+                    turned_bank[c][:, t * P : (t + 1) * P], term[:, c * CHUNK : (c + 1) * CHUNK], ident[:],
                     start=first, stop=last, is_transpose=True,
                 )
 
@@ -168,64 +178,69 @@ def tile_picked_joinoddstwicehopg_none_po_kernel(
 
         def second_hop(t):
             nc.vector.tensor_scalar(hop2[t][:], win_b[t][:].indirect(list4[:]), -1.0 / 3.0, 0.0, ALU.mult, ALU.add)
-            turn(win_a[t][:, :S], t, True, False)
-            turn(win_b[t][:, :S], t, False, False)
-            turn(hop2[t][:], t, False, True)
+            turn_and_add(win_a[t][:, :S], t, True, False)
+            turn_and_add(win_b[t][:, :S], t, False, False)
+            turn_and_add(hop2[t][:], t, False, True)
 
         def add_up(t):
             nc.gpsimd.tensor_tensor(sums[:, t, :], ex[t], ex1[t][:], ALU.add)
             nc.gpsimd.tensor_tensor(sums[:, PACK + t, :], ex2[t][:], ex3[t][:], ALU.add)
 
-        copy_y(0)
-        copy_y(1)
         for t in range(SHARED):
-            scalar_side(t)
+            copy_y(t)
+        for t in range(SHARED):
+            exponentials(t)
             first_hop(t)
             nc.vector.tensor_copy(ex3[t][:], win_e[t][:].indirect(list3[:]))
             second_hop(t)
-            copy_y(t + 2)
+            copy_y(t + SHARED)
             add_up(t)
         for t in range(SHARED, PACK):
-            scalar_side(t)
+            exponentials(t)
             first_hop(t)
         for t in range(SHARED, PACK):
             second_hop(t)
             add_up(t)
 
-        deal(w23_plane[:], w23_scale_raw[:])
+        deal_bytes(w23_bytes[:], w23_scale_raw[:])
         warm = sb("warm", [P, 2], F32)
         nc.scalar.activation(warm[:, 0:1], ex3[PACK - 1][:, 0:1], ACT.Ln)
 
-        z2_bf = sb("z2_bf", [P, S * PACK], BF16)
+        z2_bf = []
         z2_codes = sb("z2_codes", [P, S], U32)
-        z2_plane = sb("z2_plane", [P, S], U8)
-        z2t = [sb("z2t%d" % c, [P, 2, P, 2], BF16) for c in range(CHUNKS)]
+        z2_bytes = sb("z2_bytes", [P, S], U8)
+        z2_turned = [sb("z2_turned%d" % c, [P, 2, P, 2], BF16) for c in range(CHUNKS)]
         for c in range(CHUNKS):
             nc.vector.tensor_tensor(
-                z2t[c][:], z2t_bank[c][:].rearrange("j (u e p) -> j u p e", u=2, e=2), gm_row[:], ALU.mult
+                z2_turned[c][:], turned_bank[c][:].rearrange("j (u e p) -> j u p e", u=2, e=2), gm_row[:], ALU.mult
             )
 
         def turn_back(half):
-            word_bank = bank(4 + 2 * half, "word_bank%d" % half)
+            pair_bank = bank(PACK + 2 * half, "pair_bank%d" % half)
             for c in range(2):
-                pairs = z2t[2 * half + c][:].rearrange("j u p e -> j (u p e)").bitcast(F32)
+                pairs = z2_turned[2 * half + c][:].rearrange("j u p e -> j (u p e)").bitcast(F32)
                 for u in range(2):
                     at = (2 * c + u) * P
-                    nc.tensor.transpose(word_bank[:, at : at + P], pairs[:, u * P : (u + 1) * P], ident[:])
-            wide = slice(half * 1024, (half + 1) * 1024)
+                    nc.tensor.transpose(pair_bank[:, at : at + P], pairs[:, u * P : (u + 1) * P], ident[:])
+            z2_bf.append(sb("z2_bf%d" % half, [P, HALF * PACK], BF16, tag="logs%d" % half))
             nc.scalar.copy(
-                z2_bf[:, wide].bitcast(F32).rearrange("p (c j u) -> p c j u", c=2, u=2),
-                word_bank[:].rearrange("p (c u j) -> p c j u", c=2, u=2),
+                z2_bf[half][:].bitcast(F32).rearrange("p (c j u) -> p c j u", c=2, u=2),
+                pair_bank[:].rearrange("p (c u j) -> p c j u", c=2, u=2),
             )
 
-        def quantize_z2(half):
-            wide = slice(half * 1024, (half + 1) * 1024)
-            cols = slice(half * 256, (half + 1) * 256)
-            nc.vector.quantize_mx(out=z2_codes[:, cols].bitcast(FP8X4), scales=z2_plane[:, cols], in_=z2_bf[:, wide])
+        def multiply_z2(half):
+            cols = slice(half * HALF, (half + 1) * HALF)
+            nc.vector.quantize_mx(out=z2_codes[:, cols].bitcast(FP8X4), scales=z2_bytes[:, cols], in_=z2_bf[half][:])
+            for t in range(PACK):
+                rows = slice(t * P, (t + 1) * P)
+                nc.tensor.matmul_mx(
+                    out=h_bank[t][:, cols], lhsT=w3_codes[:, rows].bitcast(FP8X4), lhsT_scale=w23_bytes[4:, rows],
+                    rhs=z2_codes[:, cols].bitcast(FP8X4), rhs_scale=z2_bytes[:, cols], start=(half == 0), stop=False,
+                )
 
         z_bf = sb("z_bf", [P, S * PACK], BF16)
         z_codes = sb("z_codes", [P, S], U32)
-        z_plane = sb("z_plane", [P, S], U8)
+        z_bytes = sb("z_bytes", [P, S], U8)
         h_bank = [bank(t, "h_bank%d" % t) for t in range(PACK)]
         logs = [sb("logs%d" % c, [P, 2 * PACK, CHUNK], F32) for c in range(CHUNKS)]
         odds = [sb("odds%d" % c, [P, PACK, CHUNK], F32) for c in range(CHUNKS)]
@@ -238,82 +253,96 @@ def tile_picked_joinoddstwicehopg_none_po_kernel(
 
         def gain_z(c):
             nc.vector.tensor_tensor(
-                z_bf[:, c * CHUNK * PACK : (c + 1) * CHUNK * PACK].rearrange("p (c i t) -> p c t i", i=4, t=PACK),
-                odds[c][:].rearrange("p t (c i) -> p c t i", i=4),
-                gn_wide[:].rearrange("p t (c i) -> p c t i", i=4),
+                interleaved(z_bf[:, c * CHUNK * PACK : (c + 1) * CHUNK * PACK]), by_runs(odds[c][:]),
+                by_runs(gn_wide[:]),
                 ALU.mult,
             )
 
-        def multiply(c):
+        def multiply_z(c):
             cols = slice(c * CHUNK, (c + 1) * CHUNK)
             wide = slice(c * CHUNK * PACK, (c + 1) * CHUNK * PACK)
-            nc.vector.quantize_mx(out=z_codes[:, cols].bitcast(FP8X4), scales=z_plane[:, cols], in_=z_bf[:, wide])
+            nc.vector.quantize_mx(out=z_codes[:, cols].bitcast(FP8X4), scales=z_bytes[:, cols], in_=z_bf[:, wide])
             for t in range(PACK):
                 rows = slice(t * P, (t + 1) * P)
                 nc.tensor.matmul_mx(
-                    out=h_bank[t][:, cols], lhsT=w3_codes[:, rows].bitcast(FP8X4), lhsT_scale=w23_plane[4:, rows],
-                    rhs=z2_codes[:, cols].bitcast(FP8X4), rhs_scale=z2_plane[:, cols], start=True, stop=False,
-                )
-                nc.tensor.matmul_mx(
-                    out=h_bank[t][:, cols], lhsT=w2_codes[:, rows].bitcast(FP8X4), lhsT_scale=w23_plane[:, rows],
-                    rhs=z_codes[:, cols].bitcast(FP8X4), rhs_scale=z_plane[:, cols], start=False, stop=True,
+                    out=h_bank[t][:, cols], lhsT=w2_codes[:, rows].bitcast(FP8X4), lhsT_scale=w23_bytes[:, rows],
+                    rhs=z_codes[:, cols].bitcast(FP8X4), rhs_scale=z_bytes[:, cols],
+                    start=False, stop=(c == CHUNKS - 1),
                 )
 
         take_logs(0)
-        turn_back(0)
         subtract_logs(0)
         take_logs(1)
-        quantize_z2(0)
+        turn_back(0)
         gain_z(0)
-        turn_back(1)
         subtract_logs(1)
-        multiply(0)
         take_logs(2)
+        multiply_z2(0)
+        multiply_z(0)
+        turn_back(1)
         gain_z(1)
-        quantize_z2(1)
-        multiply(1)
         subtract_logs(2)
+        multiply_z(1)
         take_logs(3)
+        multiply_z2(1)
         gain_z(2)
         subtract_logs(3)
-        multiply(2)
+        multiply_z(2)
         gain_z(3)
-        multiply(3)
+        multiply_z(3)
 
         nc.scalar.activation(warm[:, 1:2], logs[CHUNKS - 1][:, 0, 0:1], ACT.Sigmoid)
+
+        last = PACK - 1
         result = sb("result", [P, PACK, S], F32)
         out_rows = out_0.rearrange("(p t) j -> p t j", t=PACK)
         out_bf = sb("out_bf", [P, S * PACK], BF16)
         out_codes = sb("out_codes", [P, S], U32)
-        out_plane = sb("out_plane", [P, S], U8)
-        half = S // 2
-        for t in range(2):
-            nc.vector.tensor_copy(win_a[t][:, :S], h_bank[t][:])
-        for t in range(PACK):
-            if t < 2:
-                gate = win_a[t + 2][:, :S]
-            else:
-                nc.scalar.copy(win_a[t][:, :S], h_bank[t][:])
-                gate = win_a[t - 2][:, :S]
-            nc.scalar.activation(gate, win_a[t][:].indirect(list5[:]), ACT.Sigmoid)
-            st2 = win_b[t][:, :S]
-            nc.vector.tensor_tensor(st2, h_bank[t][:], gate, ALU.mult)
-            other = sb("other%d" % t, [P, S], F32)
-            for lo, hi in ((0, S),) if t < PACK - 1 else ((0, half), (half, S)):
-                nc.vector.tensor_copy(other[:, lo:hi], win_b[t][:].indirect(list6[:, lo // 16 : hi // 16]))
-                (nc.gpsimd if t < PACK - 1 else nc.vector).tensor_tensor(result[:, t, lo:hi], st2[:, lo:hi], other[:, lo:hi], ALU.subtract)
-                nc.sync.dma_start(out_rows[:, t, lo:hi], result[:, t, lo:hi])
+        out_bytes = sb("out_bytes", [P, S], U8)
+        gate = [win_a[last][:, :S], win_e[0][:, :S], win_e[1][:, :S], win_a[0][:, :S]]
+        other = [sb("other%d" % t, [P, S], F32) for t in range(PACK)]
 
-        for copy, lo, hi in ((nc.scalar.copy, 0, half), (nc.vector.tensor_copy, half, S)):
-            copy(
-                out_bf[:, lo * PACK : hi * PACK].rearrange("p (c i t) -> p c t i", i=4, t=PACK),
-                result[:, :, lo:hi].rearrange("p t (c i) -> p c t i", i=4),
-            )
-        for lo, hi in ((0, half), (half, S)):
+        def sigmoid_of_h(t):
+            nc.scalar.activation(gate[t], win_a[t][:].indirect(list5[:]), ACT.Sigmoid)
+
+        def gate_h(t):
+            nc.vector.tensor_tensor(win_b[t][:, :S], h_bank[t][:], gate[t], ALU.mult)
+
+        def fetch(t, lo, hi):
+            nc.vector.tensor_copy(other[t][:, lo:hi], win_b[t][:].indirect(list6[:, lo // 16 : hi // 16]))
+
+        def finish(engine, t, lo, hi):
+            engine.tensor_tensor(result[:, t, lo:hi], win_b[t][:, lo:hi], other[t][:, lo:hi], ALU.subtract)
+            nc.sync.dma_start(out_rows[:, t, lo:hi], result[:, t, lo:hi])
+
+        for t in range(last):
+            nc.vector.tensor_copy(win_a[t][:, :S], h_bank[t][:])
+            sigmoid_of_h(t)
+        gate_h(0)
+        nc.scalar.copy(win_a[last][:, :S], h_bank[last][:])
+        sigmoid_of_h(last)
+        fetch(0, 0, S)
+        finish(nc.gpsimd, 0, 0, S)
+        gate_h(1)
+        gate_h(2)
+        fetch(1, 0, S)
+        finish(nc.gpsimd, 1, 0, S)
+        gate_h(last)
+        fetch(2, 0, S)
+        finish(nc.gpsimd, 2, 0, S)
+        halves = ((0, HALF), (HALF, S))
+        for lo, hi in halves:
+            fetch(last, lo, hi)
+        for lo, hi in halves:
+            finish(nc.vector, last, lo, hi)
+
+        for copy, (lo, hi) in zip((nc.scalar.copy, nc.vector.tensor_copy), halves):
+            copy(interleaved(out_bf[:, lo * PACK : hi * PACK]), by_runs(result[:, :, lo:hi]))
+        for lo, hi in halves:
             nc.vector.quantize_mx(
-                out=out_codes[:, lo:hi].bitcast(FP8X4), scales=out_plane[:, lo:hi], in_=out_bf[:, lo * PACK : hi * PACK]
+                out=out_codes[:, lo:hi].bitcast(FP8X4), scales=out_bytes[:, lo:hi], in_=out_bf[:, lo * PACK : hi * PACK]
             )
             nc.scalar.dma_start(words_of(out_1)[:, lo:hi], out_codes[:, lo:hi].bitcast(I32))
         for q in range(4):
             queue = nc.scalar if q % 2 else nc.sync
-            queue.dma_start(out_2[0, 4 * q : 4 * q + 4, :].bitcast(I32), out_plane[32 * q : 32 * q + 4, :].bitcast(I32))
+            queue.dma_start(out_2[0, 4 * q : 4 * q + 4, :].bitcast(I32), out_bytes[32 * q : 32 * q + 4, :].bitcast(I32))

from contextlib import ExitStack

import concourse.mybir as mybir
from concourse.masks import make_identity

K, T, S, H, N = 512, 2048, 512, 512, 512
FLOPS = 2 * S * (K * H + 2 * H * N)

F32 = mybir.dt.float32
BF16 = mybir.dt.bfloat16
I32 = mybir.dt.int32
U32 = mybir.dt.uint32
U16 = mybir.dt.uint16
U8 = mybir.dt.uint8
FP8X4 = mybir.dt.float8_e4m3fn_x4
ACT = mybir.ActivationFunctionType
ALU = mybir.AluOpType

P = 128
PACK = 4
CHUNK = 128
CHUNKS = S // CHUNK
HALF = S // 2
RUN = 4
SHARED = 2


def words_of(dram):
    return dram[0].rearrange("p n t -> p (n t)").bitcast(I32)


def interleaved(tile):
    return tile.rearrange("p (c i t) -> p c t i", i=RUN, t=PACK)


def by_runs(quarters):
    return quarters.rearrange("p t (c i) -> p c t i", i=RUN)


def tile_picked_joinoddstwicehopg_none_po_kernel(
    tc, x_words, x_scales, w1_words, w1_scales, gn, gm, w2_words, w2_scales, w3_words, w3_scales,
    offs, n1, n2, n3, n4, n5, n6, out_0, out_1, out_2,
):
    nc = tc.nc
    with ExitStack() as ctx:
        lists = ctx.enter_context(tc.tile_pool(name="lists", bufs=1))
        keep = ctx.enter_context(tc.tile_pool(name="keep", bufs=1))
        psum = ctx.enter_context(tc.psum_pool(name="psum", bufs=1))

        def sb(name, shape, dtype, tag=""):
            return keep.tile(shape, dtype, name=name, tag=tag or name, align_bytes=64)

        def bank(index, name):
            return psum.tile([P, 512], F32, name=name, tag="bank%d" % index)

        def load_list(name, dram):
            held = lists.tile([P, S // 16], U16, name=name)
            nc.sync.dma_start(held[:], dram)
            return held

        def load_scales(tile, first_row, dram):
            for q in range(4):
                rows = slice(32 * q + first_row, 32 * q + first_row + 4)
                nc.sync.dma_start(tile[rows, :].bitcast(I32), dram[0, 4 * q : 4 * q + 4, :].bitcast(I32))

        def deal(dealt, raw):
            nc.vector.tensor_copy(
                out=dealt.rearrange("p (t m) -> p t m", t=PACK), in_=raw.rearrange("p (m t) -> p t m", t=PACK)
            )

        def deal_bytes(dealt, raw):
            nc.vector.tensor_copy(
                out=dealt.rearrange("p (t m) -> p m t", t=PACK), in_=raw.rearrange("p (m t) -> p m t", t=PACK)
            )

        x_scale_table = sb("x_scale_table", [P, T], U8)
        w1_scale_raw = sb("w1_scale_raw", [P, H], U8)
        w23_scale_raw = sb("w23_scale_raw", [P, N], U8)
        nc.vector.memset(x_scale_table[:].bitcast(I32), 0)
        nc.vector.memset(w1_scale_raw[:].bitcast(I32), 0)
        nc.vector.memset(w23_scale_raw[:].bitcast(I32), 0)
        ident = sb("ident", [P, P], F32)
        make_identity(nc, ident[:])

        picks = load_list("picks", offs)
        x_table = sb("x_table", [P, T], I32)
        nc.sync.dma_start(x_table[:], words_of(x_words))
        load_scales(x_scale_table, 0, x_scales)
        w1_raw = sb("w1_raw", [P, H], I32)
        nc.sync.dma_start(w1_raw[:], words_of(w1_words))
        load_scales(w1_scale_raw, 0, w1_scales)
        list4 = load_list("list4", n4)
        list1 = load_list("list1", n1)
        list2 = load_list("list2", n2)
        list3 = load_list("list3", n3)
        w2_raw = sb("w2_raw", [P, N], I32)
        w3_raw = sb("w3_raw", [P, N], I32)
        nc.sync.dma_start(w2_raw[:], words_of(w2_words))
        nc.sync.dma_start(w3_raw[:], words_of(w3_words))
        gn_cols = sb("gn_cols", [P, PACK], F32)
        gm_cols = sb("gm_cols", [P, PACK], F32)
        nc.gpsimd.dma_start(gm_cols[:], gm.rearrange("(p t) o -> p (t o)", t=PACK))
        nc.gpsimd.dma_start(gn_cols[:], gn.rearrange("(p t) o -> p (t o)", t=PACK))
        list5 = load_list("list5", n5)
        list6 = load_list("list6", n6)
        load_scales(w23_scale_raw, 0, w2_scales)
        load_scales(w23_scale_raw, 4, w3_scales)

        win_a = [sb("win_a%d" % t, [P, 2 * S], F32) for t in range(PACK)]
        win_b = [sb("win_b%d" % t, [P, 2 * S], F32) for t in range(PACK)]
        win_e = [sb("win_e%d" % t, [P, 2 * S], F32) for t in range(SHARED)]
        for t in range(SHARED):
            nc.vector.memset(win_a[t][:, S:], 0.0)
            nc.vector.memset(win_e[t][:, S:], 0.0)
        for t in range(PACK):
            nc.gpsimd.memset(win_b[t][:, S:], 0.0)

        w1_codes = sb("w1_codes", [P, H], I32)
        w1_bytes = sb("w1_bytes", [P, H], U8)
        deal(w1_codes[:], w1_raw[:])
        deal_bytes(w1_bytes[:], w1_scale_raw[:])

        x_codes = sb("x_codes", [P, S], U32)
        x_bytes = sb("x_bytes", [P, S], U8)
        nc.vector.tensor_copy(x_bytes[:], x_scale_table[:].indirect(picks[:]))
        nc.vector.tensor_copy(x_codes[:], x_table[:].bitcast(U32).indirect(picks[:]))

        y_bank = [bank(t, "y_bank%d" % t) for t in range(PACK)]
        for t in range(PACK):
            rows = slice(t * P, (t + 1) * P)
            nc.tensor.matmul_mx(
                out=y_bank[t][:], lhsT=w1_codes[:, rows].bitcast(FP8X4), lhsT_scale=w1_bytes[:, rows],
                rhs=x_codes[:].bitcast(FP8X4), rhs_scale=x_bytes[:], start=True, stop=True,
            )

        w2_codes = sb("w2_codes", [P, N], I32)
        w3_codes = sb("w3_codes", [P, N], I32)
        w23_bytes = sb("w23_bytes", [P, N], U8)
        deal(w2_codes[:], w2_raw[:])
        deal(w3_codes[:], w3_raw[:])

        gn_wide = sb("gn_wide", [P, PACK, CHUNK], F32)
        for t in range(PACK):
            nc.vector.tensor_copy(gn_wide[:, t, :], gn_cols[:, t : t + 1].to_broadcast([P, CHUNK]))
        gm_bank = bank(4, "gm_bank")
        for t in range(PACK):
            nc.tensor.transpose(gm_bank[:, t * P : (t + 1) * P], gm_cols[:, t : t + 1].to_broadcast([P, P]), ident[:])
        gm_row = sb("gm_row", [P, 2, P, 2], F32)
        nc.scalar.copy(gm_row[:], gm_bank[:].rearrange("j (u e p) -> j u p e", u=2, e=2))

        sums = sb("sums", [P, 2 * PACK, S], F32)
        turned_bank = [bank(PACK + c, "turned_bank%d" % c) for c in range(CHUNKS)]
        ex1 = [sb("ex1_%d" % t, [P, S], F32) for t in range(PACK)]
        ex2 = [sb("ex2_%d" % t, [P, S], F32) for t in range(PACK)]
        ex3 = [sb("ex3_%d" % t, [P, S], F32) for t in range(PACK)]
        hop2 = [sb("hop2_%d" % t, [P, S], F32) for t in range(PACK)]
        ex = [win_e[t][:, :S] if t < SHARED else win_a[t][:, S:] for t in range(PACK)]

        def copy_y(t):
            nc.vector.tensor_copy(win_a[t][:, :S], y_bank[t][:])

        def exponentials(t):
            nc.scalar.activation(ex[t], y_bank[t][:], ACT.Exp, scale=0.5)
            nc.scalar.activation(ex1[t][:], win_a[t][:].indirect(list1[:]), ACT.Exp, scale=0.5)
            nc.scalar.activation(ex2[t][:], win_a[t][:].indirect(list2[:]), ACT.Exp, scale=0.5)
            if t >= SHARED:
                nc.scalar.activation(ex3[t][:], win_a[t][:].indirect(list3[:]), ACT.Exp, scale=0.5)

        def turn_and_add(term, t, first, last):
            for c in range(CHUNKS):
                nc.tensor.matmul(
                    turned_bank[c][:, t * P : (t + 1) * P], term[:, c * CHUNK : (c + 1) * CHUNK], ident[:],
                    start=first, stop=last, is_transpose=True,
                )

        def first_hop(t):
            nc.vector.tensor_scalar(win_b[t][:, :S], win_a[t][:].indirect(list4[:]), -1.5, 0.0, ALU.mult, ALU.add)

        def second_hop(t):
            nc.vector.tensor_scalar(hop2[t][:], win_b[t][:].indirect(list4[:]), -1.0 / 3.0, 0.0, ALU.mult, ALU.add)
            turn_and_add(win_a[t][:, :S], t, True, False)
            turn_and_add(win_b[t][:, :S], t, False, False)
            turn_and_add(hop2[t][:], t, False, True)

        def add_up(t):
            nc.gpsimd.tensor_tensor(sums[:, t, :], ex[t], ex1[t][:], ALU.add)
            nc.gpsimd.tensor_tensor(sums[:, PACK + t, :], ex2[t][:], ex3[t][:], ALU.add)

        for t in range(SHARED):
            copy_y(t)
        for t in range(SHARED):
            exponentials(t)
            first_hop(t)
            nc.vector.tensor_copy(ex3[t][:], win_e[t][:].indirect(list3[:]))
            second_hop(t)
            copy_y(t + SHARED)
            add_up(t)
        for t in range(SHARED, PACK):
            exponentials(t)
            first_hop(t)
        for t in range(SHARED, PACK):
            second_hop(t)
            add_up(t)

        deal_bytes(w23_bytes[:], w23_scale_raw[:])
        warm = sb("warm", [P, 2], F32)
        nc.scalar.activation(warm[:, 0:1], ex3[PACK - 1][:, 0:1], ACT.Ln)

        z2_bf = []
        z2_codes = sb("z2_codes", [P, S], U32)
        z2_bytes = sb("z2_bytes", [P, S], U8)
        z2_turned = [sb("z2_turned%d" % c, [P, 2, P, 2], BF16) for c in range(CHUNKS)]
        for c in range(CHUNKS):
            nc.vector.tensor_tensor(
                z2_turned[c][:], turned_bank[c][:].rearrange("j (u e p) -> j u p e", u=2, e=2), gm_row[:], ALU.mult
            )

        def turn_back(half):
            pair_bank = bank(PACK + 2 * half, "pair_bank%d" % half)
            for c in range(2):
                pairs = z2_turned[2 * half + c][:].rearrange("j u p e -> j (u p e)").bitcast(F32)
                for u in range(2):
                    at = (2 * c + u) * P
                    nc.tensor.transpose(pair_bank[:, at : at + P], pairs[:, u * P : (u + 1) * P], ident[:])
            z2_bf.append(sb("z2_bf%d" % half, [P, HALF * PACK], BF16, tag="logs%d" % half))
            nc.scalar.copy(
                z2_bf[half][:].bitcast(F32).rearrange("p (c j u) -> p c j u", c=2, u=2),
                pair_bank[:].rearrange("p (c u j) -> p c j u", c=2, u=2),
            )

        def multiply_z2(half):
            cols = slice(half * HALF, (half + 1) * HALF)
            nc.vector.quantize_mx(out=z2_codes[:, cols].bitcast(FP8X4), scales=z2_bytes[:, cols], in_=z2_bf[half][:])
            for t in range(PACK):
                rows = slice(t * P, (t + 1) * P)
                nc.tensor.matmul_mx(
                    out=h_bank[t][:, cols], lhsT=w3_codes[:, rows].bitcast(FP8X4), lhsT_scale=w23_bytes[4:, rows],
                    rhs=z2_codes[:, cols].bitcast(FP8X4), rhs_scale=z2_bytes[:, cols], start=(half == 0), stop=False,
                )

        z_bf = sb("z_bf", [P, S * PACK], BF16)
        z_codes = sb("z_codes", [P, S], U32)
        z_bytes = sb("z_bytes", [P, S], U8)
        h_bank = [bank(t, "h_bank%d" % t) for t in range(PACK)]
        logs = [sb("logs%d" % c, [P, 2 * PACK, CHUNK], F32) for c in range(CHUNKS)]
        odds = [sb("odds%d" % c, [P, PACK, CHUNK], F32) for c in range(CHUNKS)]

        def take_logs(c):
            nc.scalar.activation(logs[c][:], sums[:, :, c * CHUNK : (c + 1) * CHUNK], ACT.Ln)

        def subtract_logs(c):
            nc.vector.tensor_tensor(odds[c][:], logs[c][:, :PACK, :], logs[c][:, PACK:, :], ALU.subtract)

        def gain_z(c):
            nc.vector.tensor_tensor(
                interleaved(z_bf[:, c * CHUNK * PACK : (c + 1) * CHUNK * PACK]), by_runs(odds[c][:]),
                by_runs(gn_wide[:]),
                ALU.mult,
            )

        def multiply_z(c):
            cols = slice(c * CHUNK, (c + 1) * CHUNK)
            wide = slice(c * CHUNK * PACK, (c + 1) * CHUNK * PACK)
            nc.vector.quantize_mx(out=z_codes[:, cols].bitcast(FP8X4), scales=z_bytes[:, cols], in_=z_bf[:, wide])
            for t in range(PACK):
                rows = slice(t * P, (t + 1) * P)
                nc.tensor.matmul_mx(
                    out=h_bank[t][:, cols], lhsT=w2_codes[:, rows].bitcast(FP8X4), lhsT_scale=w23_bytes[:, rows],
                    rhs=z_codes[:, cols].bitcast(FP8X4), rhs_scale=z_bytes[:, cols],
                    start=False, stop=(c == CHUNKS - 1),
                )

        take_logs(0)
        subtract_logs(0)
        take_logs(1)
        turn_back(0)
        gain_z(0)
        subtract_logs(1)
        take_logs(2)
        multiply_z2(0)
        multiply_z(0)
        turn_back(1)
        gain_z(1)
        subtract_logs(2)
        multiply_z(1)
        take_logs(3)
        multiply_z2(1)
        gain_z(2)
        subtract_logs(3)
        multiply_z(2)
        gain_z(3)
        multiply_z(3)

        nc.scalar.activation(warm[:, 1:2], logs[CHUNKS - 1][:, 0, 0:1], ACT.Sigmoid)

        last = PACK - 1
        result = sb("result", [P, PACK, S], F32)
        out_rows = out_0.rearrange("(p t) j -> p t j", t=PACK)
        out_bf = sb("out_bf", [P, S * PACK], BF16)
        out_codes = sb("out_codes", [P, S], U32)
        out_bytes = sb("out_bytes", [P, S], U8)
        gate = [win_a[last][:, :S], win_e[0][:, :S], win_e[1][:, :S], win_a[0][:, :S]]
        other = [sb("other%d" % t, [P, S], F32) for t in range(PACK)]

        def sigmoid_of_h(t):
            nc.scalar.activation(gate[t], win_a[t][:].indirect(list5[:]), ACT.Sigmoid)

        def gate_h(t):
            nc.vector.tensor_tensor(win_b[t][:, :S], h_bank[t][:], gate[t], ALU.mult)

        def fetch(t, lo, hi):
            nc.vector.tensor_copy(other[t][:, lo:hi], win_b[t][:].indirect(list6[:, lo // 16 : hi // 16]))

        def finish(engine, t, lo, hi):
            engine.tensor_tensor(result[:, t, lo:hi], win_b[t][:, lo:hi], other[t][:, lo:hi], ALU.subtract)
            nc.sync.dma_start(out_rows[:, t, lo:hi], result[:, t, lo:hi])

        for t in range(last):
            nc.vector.tensor_copy(win_a[t][:, :S], h_bank[t][:])
            sigmoid_of_h(t)
        gate_h(0)
        nc.scalar.copy(win_a[last][:, :S], h_bank[last][:])
        sigmoid_of_h(last)
        fetch(0, 0, S)
        finish(nc.gpsimd, 0, 0, S)
        gate_h(1)
        gate_h(2)
        fetch(1, 0, S)
        finish(nc.gpsimd, 1, 0, S)
        gate_h(last)
        fetch(2, 0, S)
        finish(nc.gpsimd, 2, 0, S)
        halves = ((0, HALF), (HALF, S))
        for lo, hi in halves:
            fetch(last, lo, hi)
        for lo, hi in halves:
            finish(nc.vector, last, lo, hi)

        for copy, (lo, hi) in zip((nc.scalar.copy, nc.vector.tensor_copy), halves):
            copy(interleaved(out_bf[:, lo * PACK : hi * PACK]), by_runs(result[:, :, lo:hi]))
        for lo, hi in halves:
            nc.vector.quantize_mx(
                out=out_codes[:, lo:hi].bitcast(FP8X4), scales=out_bytes[:, lo:hi], in_=out_bf[:, lo * PACK : hi * PACK]
            )
            nc.scalar.dma_start(words_of(out_1)[:, lo:hi], out_codes[:, lo:hi].bitcast(I32))
        for q in range(4):
            queue = nc.scalar if q % 2 else nc.sync
            queue.dma_start(out_2[0, 4 * q : 4 * q + 4, :].bitcast(I32), out_bytes[32 * q : 32 * q + 4, :].bitcast(I32))
